import numpy as np
import ml_dtypes


def mxq(x, axis, fmt="e4m3"):
    dtype, down = {"e4m3": (ml_dtypes.float8_e4m3fn, 7), "e5m2": (ml_dtypes.float8_e5m2, 14)}[fmt]
    v = np.moveaxis(np.asarray(x, np.float32).astype(ml_dtypes.bfloat16).astype(np.float64), axis, -1)
    blocks = v.reshape(v.shape[:-1] + (-1, 32))
    amax = np.abs(blocks).max(-1, keepdims=True)
    byte = np.maximum(np.where(amax > 0, np.frexp(amax)[1] - 1 + 127, 0) - down, 1)
    scale = np.exp2(byte - 127.0)
    codes = (blocks / scale).astype(np.float32).astype(dtype).astype(np.float64)
    return np.moveaxis((codes * scale).reshape(v.shape), -1, axis)


WIDE = False


def mx_kscale(k):
    if not WIDE:
        return np.ones(k)
    levels = np.array([10, -10, 5, -5, 0])
    if k % 512:
        return np.exp2(np.random.permutation(np.resize(levels, k // 32))).repeat(32)
    a = np.empty((k // 512, 16))
    for p in range(k // 512):
        a[p, :8] = np.random.permutation(np.resize(levels, 8))
        for g in range(8):
            far = levels[np.abs(levels - a[p, g]) >= 10]
            a[p, g + 8] = far[np.random.randint(len(far))]
    return np.exp2(a.ravel()).repeat(32)


def f64(x):
    return np.asarray(x).astype(np.float64)


def striped(idx):
    return np.tile(np.asarray(idx).reshape(-1, 16).T, (8, 1)).astype(np.uint16)


def unstriped(offs):
    return offs[:16].T.reshape(-1).astype(np.int64)


def striped8(idx):
    return np.asarray(idx).reshape(8, -1, 16).transpose(0, 2, 1).reshape(128, -1).astype(np.uint16)


def unstriped8(offs):
    return offs.reshape(8, 16, -1).transpose(0, 2, 1).reshape(8, -1).astype(np.int64)


def pick8(x, idx, run):
    r = np.arange(len(x))
    return x[r[:, None], idx[r % (8 * run) // run]]


E2M1 = np.array([0.0, 0.5, 1.0, 1.5, 2.0, 3.0, 4.0, 6.0, -0.0, -0.5, -1.0, -1.5, -2.0, -3.0, -4.0, -6.0])


def pack_weight(w, fmt):
    k, n = w.shape
    w = f64(np.asarray(w, np.float32).astype(ml_dtypes.bfloat16)).reshape(k // 32, 32, n)
    amax = np.abs(w).max(1)
    if fmt == "e4m3":
        byte = np.frexp(amax)[1] - 1 + 127 - 7
    else:
        mant, ex = np.frexp(amax / 6.0)
        byte = np.where(mant > 0.5, ex, ex - 1) + 127
    byte = np.clip(np.where(amax > 0, byte, 1), 1, 254)
    scaled = (w * np.exp2(127.0 - byte)[:, None, :]).reshape(k, n).astype(np.float32)
    by_word = np.ascontiguousarray(scaled.reshape(k // 512, 128, 4, n).transpose(0, 1, 3, 2))
    if fmt == "e4m3":
        words = by_word.astype(ml_dtypes.float8_e4m3fn).view(np.uint8)
    else:
        c = by_word.astype(ml_dtypes.float4_e2m1fn).view(np.uint8) & 0xF
        words = (c[..., 0::2] | (c[..., 1::2] << 4)).reshape(k // 512, 128, 2 * n)
    return np.ascontiguousarray(words), np.ascontiguousarray(byte.astype(np.uint8).reshape(k // 512, 16, n))


def unpack_weight(words, scales, fmt):
    g, _, n = scales.shape
    words = np.ascontiguousarray(words).reshape(g, 128, n, -1)
    if fmt == "e4m3":
        vals = words.view(ml_dtypes.float8_e4m3fn).astype(np.float64)
    else:
        nib = np.empty((g, 128, n, 4), np.uint8)
        nib[..., 0::2] = words & 0xF
        nib[..., 1::2] = words >> 4
        vals = E2M1[nib]
    vals = vals * np.repeat(np.exp2(scales.astype(np.float64) - 127.0), 8, axis=1)[..., None]
    return vals.transpose(0, 1, 3, 2).reshape(g * 512, n)


def sigmoid(v):
    return 1.0 / (1.0 + np.exp(-v))


def sgn(shape):
    return np.random.uniform(0.5, 2.0, shape) * np.where(np.random.standard_normal(shape) < 0, -1.0, 1.0)


K, J, R, T, O, N, U, E = 512, 512, 512, 2048, 256, 256, 512, 128


def setup_inputs():
    n = np.random.standard_normal
    idx = np.random.permutation(T)[:J]
    idx2 = np.stack([np.random.permutation(J)[:O] for _ in range(8)])
    idx3 = np.stack([np.random.permutation(J)[:O] for _ in range(8)])
    idx4 = np.stack([np.random.permutation(U)[:O] for _ in range(8)])
    idx5 = np.stack([np.random.permutation(U)[:O] for _ in range(8)])
    idx6 = np.stack([np.random.permutation(U)[:E] for _ in range(8)])
    idx7 = np.stack([np.random.permutation(U)[:E] for _ in range(8)])
    fk = mx_kscale(K)
    fr = mx_kscale(R)
    xtp = pack_weight(n((K, T)) * fk[:, None], "e2m1")
    wp = pack_weight(n((K, R)) * 1 / np.sqrt(K) / fk[:, None] * fr, "e4m3")
    w2p = pack_weight(n((K, R)) * 1 / np.sqrt(K) / fk[:, None] * fr, "e4m3")
    wbp = pack_weight(n((R, N)) * 1 / np.sqrt(R) / fr[:, None], "e2m1")
    wop = pack_weight(n((R, N)) * 1 / np.sqrt(R) / fr[:, None], "e4m3")
    return {
        "xt_words": xtp[0],
        "xt_scales": xtp[1],
        "w_words": wp[0],
        "w_scales": wp[1],
        "w2_words": w2p[0],
        "w2_scales": w2p[1],
        "sa": (np.random.uniform(0.5, 1.6, (R, 1))).astype(np.float32),
        "sb": (np.random.uniform(0.5, 1.6, (R, 1))).astype(np.float32),
        "wb_words": wbp[0],
        "wb_scales": wbp[1],
        "wo_words": wop[0],
        "wo_scales": wop[1],
        "se": (np.random.uniform(0.5, 1.6, (N, 1))).astype(np.float32),
        "sl": (sgn((N, 1))).astype(np.float32),
        "gf": (np.random.uniform(-1.0, 1.0, (N, 1))).astype(np.float32),
        "offs": striped(idx),
        "offs2": striped8(idx2),
        "offs3": striped8(idx3),
        "offs4": striped8(idx4),
        "offs5": striped8(idx5),
        "offs6": striped8(idx6),
        "offs7": striped8(idx7),
    }


def reference(xt_words, xt_scales, w_words, w_scales, w2_words, w2_scales, sa, sb, wb_words, wb_scales, wo_words, wo_scales, se, sl, gf, offs, offs2, offs3, offs4, offs5, offs6, offs7):
    idx = unstriped(offs)
    idx2 = unstriped8(offs2)
    idx3 = unstriped8(offs3)
    idx4 = unstriped8(offs4)
    idx5 = unstriped8(offs5)
    idx6 = unstriped8(offs6)
    idx7 = unstriped8(offs7)
    xtu = unpack_weight(xt_words, xt_scales, "e2m1")
    wu = unpack_weight(w_words, w_scales, "e4m3")
    w2u = unpack_weight(w2_words, w2_scales, "e4m3")
    wbu = unpack_weight(wb_words, wb_scales, "e2m1")
    wou = unpack_weight(wo_words, wo_scales, "e4m3")
    xtidxg = xtu[:, idx]
    a = wu.T @ xtidxg
    b = w2u.T @ xtidxg
    hid = np.maximum(pick8(a, idx2, 64) * f64(sa), pick8(b, idx3, 64) * f64(sb))
    hidq = mxq(hid, 0, "e4m3")
    p = wbu.T @ hidq
    q = wou.T @ hidq
    m0 = np.zeros((N, U))
    m0[np.arange(N)[:, None], idx4[np.arange(N) % 128 // 16]] = p
    m1 = np.zeros((N, U))
    m1[np.arange(N)[:, None], idx5[np.arange(N) % 128 // 16]] = q
    y = pick8(m0, idx6, 16) * f64(se) * sigmoid(pick8(m1, idx7, 16) * f64(sl) + f64(gf))
    return y

@@ -1,0 +1,222 @@
+from contextlib import ExitStack
+
+import concourse.mybir as mybir
+
+K, J, R, T, O, N, U, E = 512, 512, 512, 2048, 256, 256, 512, 128
+FLOPS = 2 * 2 * K * R * J + 2 * 2 * R * N * O
+
+F32 = mybir.dt.float32
+BF16 = mybir.dt.bfloat16
+I32 = mybir.dt.int32
+U32 = mybir.dt.uint32
+U16 = mybir.dt.uint16
+U8 = mybir.dt.uint8
+FP8X4 = mybir.dt.float8_e4m3fn_x4
+FP4X4 = mybir.dt.float4_e2m1fn_x4
+ACT = mybir.ActivationFunctionType
+ALU = mybir.AluOpType
+
+P = 128
+PACK = 4
+HJ = J // 2
+HO = O // 2
+SPLIT = 2
+
+
+def tile_picked_tokens_plain_twin_groupmeet_outcomes_endgate_kernel(
+    tc, xt_words, xt_scales, w_words, w_scales, w2_words, w2_scales, sa, sb, wb_words, wb_scales,
+    wo_words, wo_scales, se, sl, gf, offs, offs2, offs3, offs4, offs5, offs6, offs7, out,
+):
+    nc = tc.nc
+    with ExitStack() as ctx:
+        keep = ctx.enter_context(tc.tile_pool(name="keep", bufs=1))
+        psum = ctx.enter_context(tc.psum_pool(name="psum", bufs=8))
+
+        def tile(name, shape, dtype):
+            return keep.tile(shape, dtype, name=name, align_bytes=64)
+
+        def load_list(name, src):
+            t = tile(name, list(src.shape), U16)
+            nc.sync.dma_start(t[:], src)
+            return t
+
+        def load_quadrant(queue, plane, scales, q):
+            queue.dma_start(plane[32 * q : 32 * q + 4, :].bitcast(I32), scales[0, 4 * q : 4 * q + 4, :].bitcast(I32))
+
+        def load_plane(plane, scales):
+            for q in range(4):
+                load_quadrant(nc.sync, plane, scales, q)
+
+        def load_words8(queue, words, src):
+            queue.dma_start(words[:].bitcast(I32), src[0].rearrange("p c r -> p (c r)").bitcast(I32))
+
+        def bank(name):
+            return psum.tile([P, 512], F32, name=name, tag="bank")
+
+        xs_all = tile("xs_all", [P, T], U8)
+        ws_raw = tile("ws_raw", [P, R], U8)
+        w2s_raw = tile("w2s_raw", [P, R], U8)
+        wbs = tile("wbs", [P, N], U8)
+        wos = tile("wos", [P, N], U8)
+        nc.vector.memset(xs_all[:, 0 : T // 2].bitcast(I32), 0)
+        nc.gpsimd.memset(xs_all[:, T // 2 : T].bitcast(I32), 0)
+        for plane in (ws_raw, w2s_raw, wbs, wos):
+            nc.vector.memset(plane[:].bitcast(I32), 0)
+        page0 = [tile("page0_0", [P, U], F32)]
+        page1 = [tile("page1_0", [P, U], F32)]
+        for page in page0 + page1:
+            nc.vector.memset(page[:], 0.0)
+
+        xw_all = tile("xw_all", [P, T], U16)
+        w_raw = tile("w_raw", [P, R], U32)
+        w2_raw = tile("w2_raw", [P, R], U32)
+        wb = tile("wb", [P, N], U16)
+        wo = tile("wo", [P, N], U32)
+        sa_t = tile("sa_t", [P, PACK], F32)
+        sb_t = tile("sb_t", [P, PACK], F32)
+        se_t = tile("se_t", [P, 2], F32)
+        sl_t = tile("sl_t", [P, 2], F32)
+        gf_t = tile("gf_t", [P, 2], F32)
+
+        ws_rows = tile("ws_rows", [4, 4, R // 4], I32)
+
+        l1 = load_list("l1", offs)
+        nc.scalar.dma_start(ws_rows[:], w_scales[0].bitcast(I32).rearrange("(q i) c -> i q c", i=4))
+        for q in range(4):
+            load_quadrant((nc.sync, nc.scalar)[q % 2], xs_all, xt_scales, q)
+        nc.sync.dma_start(xw_all[:].bitcast(I32), xt_words[0].bitcast(I32))
+        load_words8(nc.sync, w_raw, w_words)
+        nc.gpsimd.dma_start(sa_t[:], sa.rearrange("(p t) o -> p (t o)", t=PACK))
+        nc.gpsimd.dma_start(sb_t[:], sb.rearrange("(p t) o -> p (t o)", t=PACK))
+        load_plane(w2s_raw, w2_scales)
+        l2 = load_list("l2", offs2)
+        load_words8(nc.sync, w2_raw, w2_words)
+        nc.sync.dma_start(wb[:].bitcast(I32), wb_words[0].bitcast(I32))
+        load_words8(nc.sync, wo, wo_words)
+        load_plane(wbs, wb_scales)
+        load_plane(wos, wo_scales)
+        l3 = load_list("l3", offs3)
+        l4 = load_list("l4", offs4)
+        l5 = load_list("l5", offs5)
+        l6 = load_list("l6", offs6)
+        l7 = load_list("l7", offs7)
+        with nc.allow_non_contiguous_dma(reason="one float32 for each partition and output tile"):
+            for t, src in ((se_t, se), (sl_t, sl), (gf_t, gf)):
+                nc.sync.dma_start(t[:], src.rearrange("(c p) o -> p (c o)", p=P))
+
+        xs = tile("xs", [P, J], U8)
+        xw = tile("xw", [P, J], U16)
+        w = tile("w", [P, R], U32)
+        w2 = tile("w2", [P, R], U32)
+        ws = tile("ws", [P, R], U8)
+        w2s = tile("w2s", [P, R], U8)
+
+        def deal_bytes(dealt, raw):
+            nc.gpsimd.tensor_copy(dealt[:].rearrange("p (t m) -> p t m", t=PACK), raw[:].rearrange("p (m t) -> p t m", t=PACK))
+
+        for q in range(4):
+            nc.vector.tensor_copy(ws_raw[32 * q : 32 * q + 4, :].bitcast(I32), ws_rows[:, q, :])
+        deal_bytes(ws, ws_raw)
+        nc.vector.tensor_copy(xs[:], xs_all[:].indirect(l1[:]))
+        nc.scalar.copy(w[:, 0:P], w_raw[:, 0:R:PACK])
+        nc.scalar.copy(
+            w[:, P:R].rearrange("p (t m) -> p m t", t=PACK - 1), w_raw[:].rearrange("p (m t) -> p m t", t=PACK)[:, :, 1:PACK]
+        )
+        nc.vector.tensor_copy(xw[:, 0:HJ], xw_all[:].indirect(l1[:, 0 : HJ // 16]))
+        nc.vector.tensor_copy(xw[:, HJ:J], xw_all[:].indirect(l1[:, HJ // 16 : J // 16]))
+        deal_bytes(w2s, w2s_raw)
+        for t in range(PACK):
+            nc.gpsimd.tensor_copy(w2[:, P * t : P * (t + 1)], w2_raw[:, t:R:PACK])
+
+        def first_product(acc, words, scales, t, cols):
+            rows = slice(P * t, P * (t + 1))
+            nc.tensor.matmul_mx(
+                acc, lhsT=words[:, rows].bitcast(FP8X4), lhsT_scale=scales[:, rows],
+                rhs=xw[:, cols].bitcast(FP4X4), rhs_scale=xs[:, cols], start=True, stop=True,
+            )
+
+        a = [tile(f"a{t}", [P, J], F32) for t in range(PACK)]
+        b = [tile(f"b{t}", [P, J], F32) for t in range(PACK)]
+        for t in range(SPLIT):
+            for h, copy in ((0, nc.scalar.copy), (1, nc.vector.tensor_copy)):
+                cols = slice(HJ * h, HJ * (h + 1))
+                acc = bank(f"acc_a{t}_{h}")
+                first_product(acc[:, 0:HJ], w, ws, t, cols)
+                copy(a[t][:, cols], acc[:, 0:HJ])
+        for t in range(SPLIT, PACK):
+            acc = bank(f"acc_a{t}")
+            first_product(acc[:], w, ws, t, slice(0, J))
+            nc.vector.tensor_copy(a[t][:], acc[:])
+        for t in range(PACK):
+            acc = bank(f"acc_b{t}")
+            first_product(acc[:], w2, w2s, t, slice(0, J))
+            nc.vector.tensor_copy(b[t][:], acc[:])
+
+        ga = [tile(f"ga{pair}", [P, 2, O], F32) for pair in range(2)]
+        for t in range(PACK):
+            nc.scalar.activation(ga[t // 2][:, t % 2, :], a[t][:].indirect(l2[:]), ACT.Copy, scale=sa_t[:, t : t + 1])
+
+        codes = tile("codes", [P, O], U32)
+        hs = tile("hs", [P, O], U8)
+        pq = [[tile(f"pq{i}_{c}", [P, O], F32) for c in range(2)] for i in range(2)]
+
+        def second_product(acc, i, c, cols):
+            rows = slice(P * c, P * (c + 1))
+            lhs = wb[:, rows].bitcast(FP4X4) if i == 0 else wo[:, rows].bitcast(FP8X4)
+            nc.tensor.matmul_mx(
+                acc, lhsT=lhs, lhsT_scale=(wbs, wos)[i][:, rows],
+                rhs=codes[:, cols].bitcast(FP8X4), rhs_scale=hs[:, cols], start=True, stop=True,
+            )
+
+        def scatter(i, c, cols):
+            lst = (l4, l5)[i][:, cols.start // 16 : cols.stop // 16]
+            nc.scalar.activation((page0, page1)[i][c][:].indirect(lst), pq[i][c][:, cols], ACT.Copy)
+
+        for h in range(2):
+            cols = slice(HO * h, HO * (h + 1))
+            hid = keep.tile([P, HO, PACK], BF16, name=f"hid{h}", tag="hid", align_bytes=64)
+            gb = [keep.tile([P, 2, HO], F32, name=f"gb{pair}_{h}", tag=f"gb{pair}", align_bytes=64) for pair in range(2)]
+            for t in range(PACK):
+                nc.scalar.activation(
+                    gb[t // 2][:, t % 2, :], b[t][:].indirect(l3[:, cols.start // 16 : cols.stop // 16]),
+                    ACT.Copy, scale=sb_t[:, t : t + 1],
+                )
+            for pair in range(2):
+                nc.vector.tensor_tensor(
+                    hid[:, :, 2 * pair : 2 * pair + 2],
+                    ga[pair][:, :, cols].rearrange("p t o -> p o t"),
+                    gb[pair][:].rearrange("p t o -> p o t"), ALU.max,
+                )
+            nc.vector.quantize_mx(codes[:, cols].bitcast(FP8X4), hs[:, cols], hid[:].rearrange("p o t -> p (o t)"))
+            for i in range(2):
+                acc = bank(f"acc_pq{i}_0_{h}")
+                second_product(acc[:, 0:HO], i, 0, cols)
+                copy = nc.scalar.copy if (i, h) == (0, 0) else nc.vector.tensor_copy
+                copy(pq[i][0][:, cols], acc[:, 0:HO])
+            for i in range(2):
+                scatter(i, 0, cols)
+        for pages, tag in ((page0, "gb0"), (page1, "hid")):
+            late = keep.tile([P, U], F32, name=f"page_on_{tag}", tag=tag, align_bytes=64)
+            nc.gpsimd.memset(late[:], 0.0)
+            pages.append(late)
+        for i in range(2):
+            acc = bank(f"acc_pq{i}_1")
+            second_product(acc[:, 0:O], i, 1, slice(0, O))
+            nc.vector.tensor_copy(pq[i][1][:], acc[:, 0:O])
+
+        val = [tile(f"val{c}", [P, E], F32) for c in range(2)]
+        gate = [tile(f"gate{c}", [P, E], F32) for c in range(2)]
+        res = [tile(f"res{c}", [P, E], F32) for c in range(2)]
+
+        def finish(c):
+            nc.scalar.activation(val[c][:], page0[c][:].indirect(l6[:]), ACT.Copy, scale=se_t[:, c : c + 1])
+            nc.scalar.activation(
+                gate[c][:], page1[c][:].indirect(l7[:]), ACT.Sigmoid, bias=gf_t[:, c : c + 1], scale=sl_t[:, c : c + 1]
+            )
+            nc.vector.tensor_tensor(res[c][:], val[c][:], gate[c][:], ALU.mult)
+            nc.sync.dma_start(out[P * c : P * (c + 1), :], res[c][:])
+
+        scatter(0, 1, slice(0, O))
+        finish(0)
+        scatter(1, 1, slice(0, O))
+        finish(1)

@@ -111,6 +111,11 @@ def tile_picked_tokens_plain_twin_groupmeet_outcomes_endgate_kernel(
         ws = tile("ws", [P, R], U8)
         w2s = tile("w2s", [P, R], U8)
 
+        warm_in = tile("warm_in", [P, 1], F32)
+        warm_out = tile("warm_out", [P, 1], F32)
+        nc.vector.memset(warm_in[:], 0.0)
+        nc.scalar.activation(warm_out[:], warm_in[:], ACT.Sigmoid)
+
         def deal_bytes(dealt, raw):
             nc.gpsimd.tensor_copy(dealt[:].rearrange("p (t m) -> p t m", t=PACK), raw[:].rearrange("p (m t) -> p t m", t=PACK))
 

@@ -20,7 +20,7 @@ P = 128
 PACK = 4
 HJ = J // 2
 HO = O // 2
-SPLIT = 2
+SPLIT = 3
 
 
 def tile_picked_tokens_plain_twin_groupmeet_outcomes_endgate_kernel(
@@ -32,8 +32,8 @@ def tile_picked_tokens_plain_twin_groupmeet_outcomes_endgate_kernel(
         keep = ctx.enter_context(tc.tile_pool(name="keep", bufs=1))
         psum = ctx.enter_context(tc.psum_pool(name="psum", bufs=8))
 
-        def tile(name, shape, dtype):
-            return keep.tile(shape, dtype, name=name, align_bytes=64)
+        def tile(name, shape, dtype, tag=None):
+            return keep.tile(shape, dtype, name=name, tag=tag or name, align_bytes=64)
 
         def load_list(name, src):
             t = tile(name, list(src.shape), U16)
@@ -50,6 +50,12 @@ def tile_picked_tokens_plain_twin_groupmeet_outcomes_endgate_kernel(
         def load_words8(queue, words, src):
             queue.dma_start(words[:].bitcast(I32), src[0].rearrange("p c r -> p (c r)").bitcast(I32))
 
+        def load_by_tile(queue, name, src, tag=None):
+            t = tile(name, [P, 2], F32, tag)
+            with nc.allow_non_contiguous_dma(reason="one float32 for each partition and output tile"):
+                queue.dma_start(t[:], src.rearrange("(c p) o -> p (c o)", p=P))
+            return t
+
         def bank(name):
             return psum.tile([P, 512], F32, name=name, tag="bank")
 
@@ -62,35 +68,29 @@ def tile_picked_tokens_plain_twin_groupmeet_outcomes_endgate_kernel(
         nc.gpsimd.memset(xs_all[:, T // 2 : T].bitcast(I32), 0)
         for plane in (ws_raw, w2s_raw, wbs, wos):
             nc.vector.memset(plane[:].bitcast(I32), 0)
-        page0 = [tile("page0_0", [P, U], F32)]
-        page1 = [tile("page1_0", [P, U], F32)]
-        for page in page0 + page1:
-            nc.vector.memset(page[:], 0.0)
 
-        xw_all = tile("xw_all", [P, T], U16)
+        xw_all = keep.tile([P, T], U16, name="xw_all", tag="tokens", align_bytes=64)
         w_raw = tile("w_raw", [P, R], U32)
         w2_raw = tile("w2_raw", [P, R], U32)
         wb = tile("wb", [P, N], U16)
         wo = tile("wo", [P, N], U32)
         sa_t = tile("sa_t", [P, PACK], F32)
         sb_t = tile("sb_t", [P, PACK], F32)
-        se_t = tile("se_t", [P, 2], F32)
-        sl_t = tile("sl_t", [P, 2], F32)
-        gf_t = tile("gf_t", [P, 2], F32)
 
         ws_rows = tile("ws_rows", [4, 4, R // 4], I32)
 
         l1 = load_list("l1", offs)
         nc.scalar.dma_start(ws_rows[:], w_scales[0].bitcast(I32).rearrange("(q i) c -> i q c", i=4))
+        load_words8(nc.scalar, w_raw, w_words)
         for q in range(4):
             load_quadrant((nc.sync, nc.scalar)[q % 2], xs_all, xt_scales, q)
         nc.sync.dma_start(xw_all[:].bitcast(I32), xt_words[0].bitcast(I32))
-        load_words8(nc.sync, w_raw, w_words)
         nc.gpsimd.dma_start(sa_t[:], sa.rearrange("(p t) o -> p (t o)", t=PACK))
         nc.gpsimd.dma_start(sb_t[:], sb.rearrange("(p t) o -> p (t o)", t=PACK))
+        gf_t = load_by_tile(nc.gpsimd, "gf_t", gf)
         load_plane(w2s_raw, w2_scales)
-        l2 = load_list("l2", offs2)
         load_words8(nc.sync, w2_raw, w2_words)
+        l2 = load_list("l2", offs2)
         nc.sync.dma_start(wb[:].bitcast(I32), wb_words[0].bitcast(I32))
         load_words8(nc.sync, wo, wo_words)
         load_plane(wbs, wb_scales)
@@ -98,40 +98,44 @@ def tile_picked_tokens_plain_twin_groupmeet_outcomes_endgate_kernel(
         l3 = load_list("l3", offs3)
         l4 = load_list("l4", offs4)
         l5 = load_list("l5", offs5)
+        sl_t = load_by_tile(nc.sync, "sl_t", sl)
         l6 = load_list("l6", offs6)
         l7 = load_list("l7", offs7)
-        with nc.allow_non_contiguous_dma(reason="one float32 for each partition and output tile"):
-            for t, src in ((se_t, se), (sl_t, sl), (gf_t, gf)):
-                nc.sync.dma_start(t[:], src.rearrange("(c p) o -> p (c o)", p=P))
 
         xs = tile("xs", [P, J], U8)
         xw = tile("xw", [P, J], U16)
         w = tile("w", [P, R], U32)
         w2 = tile("w2", [P, R], U32)
         ws = tile("ws", [P, R], U8)
-        w2s = tile("w2s", [P, R], U8)
 
         warm_in = tile("warm_in", [P, 1], F32)
         warm_out = tile("warm_out", [P, 1], F32)
         nc.vector.memset(warm_in[:], 0.0)
         nc.scalar.activation(warm_out[:], warm_in[:], ACT.Sigmoid)
 
-        def deal_bytes(dealt, raw):
-            nc.gpsimd.tensor_copy(dealt[:].rearrange("p (t m) -> p t m", t=PACK), raw[:].rearrange("p (m t) -> p t m", t=PACK))
+        def deal_words(dealt, raw):
+            nc.scalar.copy(dealt[:].rearrange("p (t m) -> p m t", t=PACK), raw[:].rearrange("p (m t) -> p m t", t=PACK))
+
+        def deal_bytes(engine, dealt, raw):
+            engine.tensor_copy(dealt[:].rearrange("p (t m) -> p t m", t=PACK), raw[:].rearrange("p (m t) -> p t m", t=PACK))
 
         for q in range(4):
             nc.vector.tensor_copy(ws_raw[32 * q : 32 * q + 4, :].bitcast(I32), ws_rows[:, q, :])
-        deal_bytes(ws, ws_raw)
+        deal_bytes(nc.vector, ws, ws_raw)
         nc.vector.tensor_copy(xs[:], xs_all[:].indirect(l1[:]))
-        nc.scalar.copy(w[:, 0:P], w_raw[:, 0:R:PACK])
-        nc.scalar.copy(
-            w[:, P:R].rearrange("p (t m) -> p m t", t=PACK - 1), w_raw[:].rearrange("p (m t) -> p m t", t=PACK)[:, :, 1:PACK]
-        )
+        deal_words(w, w_raw)
         nc.vector.tensor_copy(xw[:, 0:HJ], xw_all[:].indirect(l1[:, 0 : HJ // 16]))
         nc.vector.tensor_copy(xw[:, HJ:J], xw_all[:].indirect(l1[:, HJ // 16 : J // 16]))
-        deal_bytes(w2s, w2s_raw)
+        w2s = keep.tile([P, R], U8, name="w2s", tag="tokens", align_bytes=64)
+        deal_bytes(nc.gpsimd, w2s, w2s_raw)
         for t in range(PACK):
             nc.gpsimd.tensor_copy(w2[:, P * t : P * (t + 1)], w2_raw[:, t:R:PACK])
+
+        def cleared_page(name, tag):
+            page = tile(name, [P, U], F32, tag)
+            nc.gpsimd.memset(page[:], 0.0)
+            return page
+
 
         def first_product(acc, words, scales, t, cols):
             rows = slice(P * t, P * (t + 1))
@@ -142,12 +146,18 @@ def tile_picked_tokens_plain_twin_groupmeet_outcomes_endgate_kernel(
 
         a = [tile(f"a{t}", [P, J], F32) for t in range(PACK)]
         b = [tile(f"b{t}", [P, J], F32) for t in range(PACK)]
-        for t in range(SPLIT):
-            for h, copy in ((0, nc.scalar.copy), (1, nc.vector.tensor_copy)):
-                cols = slice(HJ * h, HJ * (h + 1))
-                acc = bank(f"acc_a{t}_{h}")
-                first_product(acc[:, 0:HJ], w, ws, t, cols)
-                copy(a[t][:, cols], acc[:, 0:HJ])
+
+        def half_of_a(t, h):
+            cols = slice(HJ * h, HJ * (h + 1))
+            acc = bank(f"acc_a{t}_{h}")
+            first_product(acc[:, 0:HJ], w, ws, t, cols)
+            (nc.scalar.copy, nc.vector.tensor_copy)[h](a[t][:, cols], acc[:, 0:HJ])
+
+        half_of_a(0, 0)
+        for t in range(1, SPLIT):
+            half_of_a(t, 0)
+            half_of_a(t - 1, 1)
+        half_of_a(SPLIT - 1, 1)
         for t in range(SPLIT, PACK):
             acc = bank(f"acc_a{t}")
             first_product(acc[:], w, ws, t, slice(0, J))
@@ -157,13 +167,16 @@ def tile_picked_tokens_plain_twin_groupmeet_outcomes_endgate_kernel(
             first_product(acc[:], w2, w2s, t, slice(0, J))
             nc.vector.tensor_copy(b[t][:], acc[:])
 
-        ga = [tile(f"ga{pair}", [P, 2, O], F32) for pair in range(2)]
-        for t in range(PACK):
-            nc.scalar.activation(ga[t // 2][:, t % 2, :], a[t][:].indirect(l2[:]), ACT.Copy, scale=sa_t[:, t : t + 1])
+        ga0 = tile("ga0", [P, 2, O], F32)
+        for t in range(2):
+            nc.scalar.activation(ga0[:, t, :], a[t][:].indirect(l2[:]), ACT.Copy, scale=sa_t[:, t : t + 1])
+        page0 = [cleared_page("page0_0", "a0")]
+        page1 = [cleared_page("page1_0", "a1")]
+        se_t = load_by_tile(nc.gpsimd, "se_t", se, "w2")
 
         codes = tile("codes", [P, O], U32)
         hs = tile("hs", [P, O], U8)
-        pq = [[tile(f"pq{i}_{c}", [P, O], F32) for c in range(2)] for i in range(2)]
+        pq = [tile(f"pq{h}", [P, 4, HO], F32) for h in range(2)]
 
         def second_product(acc, i, c, cols):
             rows = slice(P * c, P * (c + 1))
@@ -173,41 +186,49 @@ def tile_picked_tokens_plain_twin_groupmeet_outcomes_endgate_kernel(
                 rhs=codes[:, cols].bitcast(FP8X4), rhs_scale=hs[:, cols], start=True, stop=True,
             )
 
-        def scatter(i, c, cols):
-            lst = (l4, l5)[i][:, cols.start // 16 : cols.stop // 16]
-            nc.scalar.activation((page0, page1)[i][c][:].indirect(lst), pq[i][c][:, cols], ACT.Copy)
+        def scatter(i, c, h):
+            lst = (l4, l5)[i][:, h * HO // 16 : (h + 1) * HO // 16]
+            nc.scalar.activation((page0, page1)[i][c][:].indirect(lst), pq[h][:, 2 * c + i, :], ACT.Copy)
 
-        for h in range(2):
+        def gather_half(h, order):
+            entries = slice(h * HO // 16, (h + 1) * HO // 16)
+            ga1 = tile(f"ga1_{h}", [P, 2, HO], F32, "ga1")
+            gb = [tile(f"gb{pair}_{h}", [P, 2, HO], F32, f"gb{pair}") for pair in range(2)]
+            for which, t in order:
+                if which == "a":
+                    nc.scalar.activation(ga1[:, t % 2, :], a[t][:].indirect(l2[:, entries]), ACT.Copy, scale=sa_t[:, t : t + 1])
+                else:
+                    nc.scalar.activation(
+                        gb[t // 2][:, t % 2, :], b[t][:].indirect(l3[:, entries]), ACT.Copy, scale=sb_t[:, t : t + 1]
+                    )
+            return ga1, gb
+
+        def quantise_half(h, ga1, gb):
             cols = slice(HO * h, HO * (h + 1))
-            hid = keep.tile([P, HO, PACK], BF16, name=f"hid{h}", tag="hid", align_bytes=64)
-            gb = [keep.tile([P, 2, HO], F32, name=f"gb{pair}_{h}", tag=f"gb{pair}", align_bytes=64) for pair in range(2)]
-            for t in range(PACK):
-                nc.scalar.activation(
-                    gb[t // 2][:, t % 2, :], b[t][:].indirect(l3[:, cols.start // 16 : cols.stop // 16]),
-                    ACT.Copy, scale=sb_t[:, t : t + 1],
-                )
-            for pair in range(2):
+            hid = tile(f"hid{h}", [P, HO, PACK], BF16, "hid")
+            for pair, ga in enumerate((ga0[:, :, cols], ga1[:])):
                 nc.vector.tensor_tensor(
-                    hid[:, :, 2 * pair : 2 * pair + 2],
-                    ga[pair][:, :, cols].rearrange("p t o -> p o t"),
+                    hid[:, :, 2 * pair : 2 * pair + 2], ga.rearrange("p t o -> p o t"),
                     gb[pair][:].rearrange("p t o -> p o t"), ALU.max,
                 )
             nc.vector.quantize_mx(codes[:, cols].bitcast(FP8X4), hs[:, cols], hid[:].rearrange("p o t -> p (o t)"))
-            for i in range(2):
-                acc = bank(f"acc_pq{i}_0_{h}")
-                second_product(acc[:, 0:HO], i, 0, cols)
-                copy = nc.scalar.copy if (i, h) == (0, 0) else nc.vector.tensor_copy
-                copy(pq[i][0][:, cols], acc[:, 0:HO])
-            for i in range(2):
-                scatter(i, 0, cols)
-        for pages, tag in ((page0, "gb0"), (page1, "hid")):
-            late = keep.tile([P, U], F32, name=f"page_on_{tag}", tag=tag, align_bytes=64)
-            nc.gpsimd.memset(late[:], 0.0)
-            pages.append(late)
-        for i in range(2):
-            acc = bank(f"acc_pq{i}_1")
-            second_product(acc[:, 0:O], i, 1, slice(0, O))
-            nc.vector.tensor_copy(pq[i][1][:], acc[:, 0:O])
+
+        def outcomes(h, first, last, copy):
+            acc = bank(f"acc_pq{h}_{first}")
+            for k in range(first, last):
+                second_product(acc[:, HO * k : HO * (k + 1)], k % 2, k // 2, slice(HO * h, HO * (h + 1)))
+            copy(pq[h][:, first:last, :].rearrange("p k o -> p (k o)"), acc[:, HO * first : HO * last])
+
+        page0.append(cleared_page("page0_1", "w2_raw"))
+        page1.append(cleared_page("page1_1", "tokens"))
+        quantise_half(0, *gather_half(0, (("a", 2), ("a", 3), ("b", 0), ("b", 1), ("b", 2), ("b", 3))))
+        held = gather_half(1, (("b", 0), ("b", 1), ("a", 2), ("a", 3), ("b", 2), ("b", 3)))
+        outcomes(0, 0, 1, nc.scalar.copy)
+        outcomes(0, 1, 4, nc.vector.tensor_copy)
+        quantise_half(1, *held)
+        outcomes(1, 0, 4, nc.vector.tensor_copy)
+        for k in range(4):
+            scatter(k % 2, k // 2, 0)
 
         val = [tile(f"val{c}", [P, E], F32) for c in range(2)]
         gate = [tile(f"gate{c}", [P, E], F32) for c in range(2)]
@@ -221,7 +242,8 @@ def tile_picked_tokens_plain_twin_groupmeet_outcomes_endgate_kernel(
             nc.vector.tensor_tensor(res[c][:], val[c][:], gate[c][:], ALU.mult)
             nc.sync.dma_start(out[P * c : P * (c + 1), :], res[c][:])
 
-        scatter(0, 1, slice(0, O))
+        for k in range(3):
+            scatter(k % 2, k // 2, 1)
         finish(0)
-        scatter(1, 1, slice(0, O))
+        scatter(1, 1, 1)
         finish(1)

@@ -21,6 +21,7 @@ PACK = 4
 HJ = J // 2
 HO = O // 2
 SPLIT = 3
+SCALAR_B = 1
 
 
 def tile_picked_tokens_plain_twin_groupmeet_outcomes_endgate_kernel(
@@ -163,9 +164,13 @@ def tile_picked_tokens_plain_twin_groupmeet_outcomes_endgate_kernel(
             first_product(acc[:], w, ws, t, slice(0, J))
             nc.vector.tensor_copy(a[t][:], acc[:])
         for t in range(PACK):
+            if t == SCALAR_B:
+                acc_for_scalar = bank("acc_for_scalar")
+                first_product(acc_for_scalar[:, 0:HJ], w2, w2s, t, slice(0, HJ))
+            cols = slice(HJ if t == SCALAR_B else 0, J)
             acc = bank(f"acc_b{t}")
-            first_product(acc[:], w2, w2s, t, slice(0, J))
-            nc.vector.tensor_copy(b[t][:], acc[:])
+            first_product(acc[:, cols], w2, w2s, t, cols)
+            nc.vector.tensor_copy(b[t][:, cols], acc[:, cols])
 
         ga0 = tile("ga0", [P, 2, O], F32)
         for t in range(2):
@@ -190,22 +195,20 @@ def tile_picked_tokens_plain_twin_groupmeet_outcomes_endgate_kernel(
             lst = (l4, l5)[i][:, h * HO // 16 : (h + 1) * HO // 16]
             nc.scalar.activation((page0, page1)[i][c][:].indirect(lst), pq[h][:, 2 * c + i, :], ACT.Copy)
 
-        def gather_half(h, order):
+        def gather_a(h, ga1, t):
             entries = slice(h * HO // 16, (h + 1) * HO // 16)
-            ga1 = tile(f"ga1_{h}", [P, 2, HO], F32, "ga1")
-            gb = [tile(f"gb{pair}_{h}", [P, 2, HO], F32, f"gb{pair}") for pair in range(2)]
-            for which, t in order:
-                if which == "a":
-                    nc.scalar.activation(ga1[:, t % 2, :], a[t][:].indirect(l2[:, entries]), ACT.Copy, scale=sa_t[:, t : t + 1])
-                else:
-                    nc.scalar.activation(
-                        gb[t // 2][:, t % 2, :], b[t][:].indirect(l3[:, entries]), ACT.Copy, scale=sb_t[:, t : t + 1]
-                    )
-            return ga1, gb
+            nc.scalar.activation(ga1[:, t % 2, :], a[t][:].indirect(l2[:, entries]), ACT.Copy, scale=sa_t[:, t : t + 1])
 
-        def quantise_half(h, ga1, gb):
+        def gather_b(h, gb, t):
+            entries = slice(h * HO // 16, (h + 1) * HO // 16)
+            nc.scalar.activation(gb[:, t % 2, :], b[t][:].indirect(l3[:, entries]), ACT.Copy, scale=sb_t[:, t : t + 1])
+
+        def pair_tile(name, tag):
+            return tile(name, [P, 2, HO], F32, tag)
+
+        def quantise_half(h, ga1, gb, tag):
             cols = slice(HO * h, HO * (h + 1))
-            hid = tile(f"hid{h}", [P, HO, PACK], BF16, "hid")
+            hid = tile(f"hid{h}", [P, HO, PACK], BF16, tag)
             for pair, ga in enumerate((ga0[:, :, cols], ga1[:])):
                 nc.vector.tensor_tensor(
                     hid[:, :, 2 * pair : 2 * pair + 2], ga.rearrange("p t o -> p o t"),
@@ -221,11 +224,26 @@ def tile_picked_tokens_plain_twin_groupmeet_outcomes_endgate_kernel(
 
         page0.append(cleared_page("page0_1", "w2_raw"))
         page1.append(cleared_page("page1_1", "tokens"))
-        quantise_half(0, *gather_half(0, (("a", 2), ("a", 3), ("b", 0), ("b", 1), ("b", 2), ("b", 3))))
-        held = gather_half(1, (("b", 0), ("b", 1), ("a", 2), ("a", 3), ("b", 2), ("b", 3)))
-        outcomes(0, 0, 1, nc.scalar.copy)
+        ga1 = pair_tile("ga1_0", "ga1")
+        gb = [pair_tile("gb0_0", "gb0"), pair_tile("gb1_0", "gb1")]
+        for t in (2, 3):
+            gather_a(0, ga1, t)
+        nc.scalar.copy(b[SCALAR_B][:, 0:HJ], acc_for_scalar[:, 0:HJ])
+        for t in range(PACK):
+            gather_b(0, gb[t // 2], t)
+        quantise_half(0, ga1, gb, "hid")
+
+        ga1 = pair_tile("ga1_1", "ga1")
+        gb = [pair_tile("gb0_1", "gb0"), pair_tile("gb1_1", "hid")]
+        for t in (0, 1):
+            gather_b(1, gb[0], t)
+        for t in (2, 3):
+            gather_a(1, ga1, t)
+        for t in (2, 3):
+            gather_b(1, gb[1], t)
+        outcomes(0, 0, 1, nc.vector.tensor_copy)
         outcomes(0, 1, 4, nc.vector.tensor_copy)
-        quantise_half(1, *held)
+        quantise_half(1, ga1, gb, "gb1")
         outcomes(1, 0, 4, nc.vector.tensor_copy)
         for k in range(4):
             scatter(k % 2, k // 2, 0)

from contextlib import ExitStack

import concourse.mybir as mybir

K, J, R, T, O, N, U, E = 512, 512, 512, 2048, 256, 256, 512, 128
FLOPS = 2 * 2 * K * R * J + 2 * 2 * R * N * O

F32 = mybir.dt.float32
BF16 = mybir.dt.bfloat16
I32 = mybir.dt.int32
U32 = mybir.dt.uint32
U16 = mybir.dt.uint16
U8 = mybir.dt.uint8
FP8X4 = mybir.dt.float8_e4m3fn_x4
FP4X4 = mybir.dt.float4_e2m1fn_x4
ACT = mybir.ActivationFunctionType
ALU = mybir.AluOpType

P = 128
PACK = 4
HJ = J // 2
HO = O // 2
SPLIT = 3
SCALAR_B = 1


def tile_picked_tokens_plain_twin_groupmeet_outcomes_endgate_kernel(
    tc, xt_words, xt_scales, w_words, w_scales, w2_words, w2_scales, sa, sb, wb_words, wb_scales,
    wo_words, wo_scales, se, sl, gf, offs, offs2, offs3, offs4, offs5, offs6, offs7, out,
):
    nc = tc.nc
    with ExitStack() as ctx:
        keep = ctx.enter_context(tc.tile_pool(name="keep", bufs=1))
        psum = ctx.enter_context(tc.psum_pool(name="psum", bufs=8))

        def tile(name, shape, dtype, tag=None):
            return keep.tile(shape, dtype, name=name, tag=tag or name, align_bytes=64)

        def load_list(name, src):
            t = tile(name, list(src.shape), U16)
            nc.sync.dma_start(t[:], src)
            return t

        def load_quadrant(queue, plane, scales, q):
            queue.dma_start(plane[32 * q : 32 * q + 4, :].bitcast(I32), scales[0, 4 * q : 4 * q + 4, :].bitcast(I32))

        def load_plane(plane, scales):
            for q in range(4):
                load_quadrant(nc.sync, plane, scales, q)

        def load_words8(queue, words, src):
            queue.dma_start(words[:].bitcast(I32), src[0].rearrange("p c r -> p (c r)").bitcast(I32))

        def load_by_tile(queue, name, src, tag=None):
            t = tile(name, [P, 2], F32, tag)
            with nc.allow_non_contiguous_dma(reason="one float32 for each partition and output tile"):
                queue.dma_start(t[:], src.rearrange("(c p) o -> p (c o)", p=P))
            return t

        def bank(name):
            return psum.tile([P, 512], F32, name=name, tag="bank")

        xs_all = tile("xs_all", [P, T], U8)
        ws_raw = tile("ws_raw", [P, R], U8)
        w2s_raw = tile("w2s_raw", [P, R], U8)
        wbs = tile("wbs", [P, N], U8)
        wos = tile("wos", [P, N], U8)
        nc.vector.memset(xs_all[:, 0 : T // 2].bitcast(I32), 0)
        nc.gpsimd.memset(xs_all[:, T // 2 : T].bitcast(I32), 0)
        for plane in (ws_raw, w2s_raw, wbs, wos):
            nc.vector.memset(plane[:].bitcast(I32), 0)

        xw_all = keep.tile([P, T], U16, name="xw_all", tag="tokens", align_bytes=64)
        w_raw = tile("w_raw", [P, R], U32)
        w2_raw = tile("w2_raw", [P, R], U32)
        wb = tile("wb", [P, N], U16)
        wo = tile("wo", [P, N], U32)
        sa_t = tile("sa_t", [P, PACK], F32)
        sb_t = tile("sb_t", [P, PACK], F32)

        ws_rows = tile("ws_rows", [4, 4, R // 4], I32)

        l1 = load_list("l1", offs)
        nc.scalar.dma_start(ws_rows[:], w_scales[0].bitcast(I32).rearrange("(q i) c -> i q c", i=4))
        load_words8(nc.scalar, w_raw, w_words)
        for q in range(4):
            load_quadrant((nc.sync, nc.scalar)[q % 2], xs_all, xt_scales, q)
        nc.sync.dma_start(xw_all[:].bitcast(I32), xt_words[0].bitcast(I32))
        nc.gpsimd.dma_start(sa_t[:], sa.rearrange("(p t) o -> p (t o)", t=PACK))
        nc.gpsimd.dma_start(sb_t[:], sb.rearrange("(p t) o -> p (t o)", t=PACK))
        gf_t = load_by_tile(nc.gpsimd, "gf_t", gf)
        load_plane(w2s_raw, w2_scales)
        load_words8(nc.sync, w2_raw, w2_words)
        l2 = load_list("l2", offs2)
        nc.sync.dma_start(wb[:].bitcast(I32), wb_words[0].bitcast(I32))
        load_words8(nc.sync, wo, wo_words)
        load_plane(wbs, wb_scales)
        load_plane(wos, wo_scales)
        l3 = load_list("l3", offs3)
        l4 = load_list("l4", offs4)
        l5 = load_list("l5", offs5)
        sl_t = load_by_tile(nc.sync, "sl_t", sl)
        l6 = load_list("l6", offs6)
        l7 = load_list("l7", offs7)

        xs = tile("xs", [P, J], U8)
        xw = tile("xw", [P, J], U16)
        w = tile("w", [P, R], U32)
        w2 = tile("w2", [P, R], U32)
        ws = tile("ws", [P, R], U8)

        warm_in = tile("warm_in", [P, 1], F32)
        warm_out = tile("warm_out", [P, 1], F32)
        nc.vector.memset(warm_in[:], 0.0)
        nc.scalar.activation(warm_out[:], warm_in[:], ACT.Sigmoid)

        def deal_words(dealt, raw):
            nc.scalar.copy(dealt[:].rearrange("p (t m) -> p m t", t=PACK), raw[:].rearrange("p (m t) -> p m t", t=PACK))

        def deal_bytes(engine, dealt, raw):
            engine.tensor_copy(dealt[:].rearrange("p (t m) -> p t m", t=PACK), raw[:].rearrange("p (m t) -> p t m", t=PACK))

        for q in range(4):
            nc.vector.tensor_copy(ws_raw[32 * q : 32 * q + 4, :].bitcast(I32), ws_rows[:, q, :])
        deal_bytes(nc.vector, ws, ws_raw)
        nc.vector.tensor_copy(xs[:], xs_all[:].indirect(l1[:]))
        deal_words(w, w_raw)
        nc.vector.tensor_copy(xw[:, 0:HJ], xw_all[:].indirect(l1[:, 0 : HJ // 16]))
        nc.vector.tensor_copy(xw[:, HJ:J], xw_all[:].indirect(l1[:, HJ // 16 : J // 16]))
        w2s = keep.tile([P, R], U8, name="w2s", tag="tokens", align_bytes=64)
        deal_bytes(nc.gpsimd, w2s, w2s_raw)
        for t in range(PACK):
            nc.gpsimd.tensor_copy(w2[:, P * t : P * (t + 1)], w2_raw[:, t:R:PACK])

        def cleared_page(name, tag):
            page = tile(name, [P, U], F32, tag)
            nc.gpsimd.memset(page[:], 0.0)
            return page


        def first_product(acc, words, scales, t, cols):
            rows = slice(P * t, P * (t + 1))
            nc.tensor.matmul_mx(
                acc, lhsT=words[:, rows].bitcast(FP8X4), lhsT_scale=scales[:, rows],
                rhs=xw[:, cols].bitcast(FP4X4), rhs_scale=xs[:, cols], start=True, stop=True,
            )

        a = [tile(f"a{t}", [P, J], F32) for t in range(PACK)]
        b = [tile(f"b{t}", [P, J], F32) for t in range(PACK)]

        def half_of_a(t, h):
            cols = slice(HJ * h, HJ * (h + 1))
            acc = bank(f"acc_a{t}_{h}")
            first_product(acc[:, 0:HJ], w, ws, t, cols)
            (nc.scalar.copy, nc.vector.tensor_copy)[h](a[t][:, cols], acc[:, 0:HJ])

        half_of_a(0, 0)
        for t in range(1, SPLIT):
            half_of_a(t, 0)
            half_of_a(t - 1, 1)
        half_of_a(SPLIT - 1, 1)
        for t in range(SPLIT, PACK):
            acc = bank(f"acc_a{t}")
            first_product(acc[:], w, ws, t, slice(0, J))
            nc.vector.tensor_copy(a[t][:], acc[:])
        for t in range(PACK):
            if t == SCALAR_B:
                acc_for_scalar = bank("acc_for_scalar")
                first_product(acc_for_scalar[:, 0:HJ], w2, w2s, t, slice(0, HJ))
            cols = slice(HJ if t == SCALAR_B else 0, J)
            acc = bank(f"acc_b{t}")
            first_product(acc[:, cols], w2, w2s, t, cols)
            nc.vector.tensor_copy(b[t][:, cols], acc[:, cols])

        ga0 = tile("ga0", [P, 2, O], F32)
        for t in range(2):
            nc.scalar.activation(ga0[:, t, :], a[t][:].indirect(l2[:]), ACT.Copy, scale=sa_t[:, t : t + 1])
        page0 = [cleared_page("page0_0", "a0")]
        page1 = [cleared_page("page1_0", "a1")]
        se_t = load_by_tile(nc.gpsimd, "se_t", se, "w2")

        codes = tile("codes", [P, O], U32)
        hs = tile("hs", [P, O], U8)
        pq = [tile(f"pq{h}", [P, 4, HO], F32) for h in range(2)]

        def second_product(acc, i, c, cols):
            rows = slice(P * c, P * (c + 1))
            lhs = wb[:, rows].bitcast(FP4X4) if i == 0 else wo[:, rows].bitcast(FP8X4)
            nc.tensor.matmul_mx(
                acc, lhsT=lhs, lhsT_scale=(wbs, wos)[i][:, rows],
                rhs=codes[:, cols].bitcast(FP8X4), rhs_scale=hs[:, cols], start=True, stop=True,
            )

        def scatter(i, c, h):
            lst = (l4, l5)[i][:, h * HO // 16 : (h + 1) * HO // 16]
            nc.scalar.activation((page0, page1)[i][c][:].indirect(lst), pq[h][:, 2 * c + i, :], ACT.Copy)

        def gather_a(h, ga1, t):
            entries = slice(h * HO // 16, (h + 1) * HO // 16)
            nc.scalar.activation(ga1[:, t % 2, :], a[t][:].indirect(l2[:, entries]), ACT.Copy, scale=sa_t[:, t : t + 1])

        def gather_b(h, gb, t):
            entries = slice(h * HO // 16, (h + 1) * HO // 16)
            nc.scalar.activation(gb[:, t % 2, :], b[t][:].indirect(l3[:, entries]), ACT.Copy, scale=sb_t[:, t : t + 1])

        def pair_tile(name, tag):
            return tile(name, [P, 2, HO], F32, tag)

        def quantise_half(h, ga1, gb, tag):
            cols = slice(HO * h, HO * (h + 1))
            hid = tile(f"hid{h}", [P, HO, PACK], BF16, tag)
            for pair, ga in enumerate((ga0[:, :, cols], ga1[:])):
                nc.vector.tensor_tensor(
                    hid[:, :, 2 * pair : 2 * pair + 2], ga.rearrange("p t o -> p o t"),
                    gb[pair][:].rearrange("p t o -> p o t"), ALU.max,
                )
            nc.vector.quantize_mx(codes[:, cols].bitcast(FP8X4), hs[:, cols], hid[:].rearrange("p o t -> p (o t)"))

        def outcomes(h, first, last, copy):
            acc = bank(f"acc_pq{h}_{first}")
            for k in range(first, last):
                second_product(acc[:, HO * k : HO * (k + 1)], k % 2, k // 2, slice(HO * h, HO * (h + 1)))
            copy(pq[h][:, first:last, :].rearrange("p k o -> p (k o)"), acc[:, HO * first : HO * last])

        page0.append(cleared_page("page0_1", "w2_raw"))
        page1.append(cleared_page("page1_1", "tokens"))
        ga1 = pair_tile("ga1_0", "ga1")
        gb = [pair_tile("gb0_0", "gb0"), pair_tile("gb1_0", "gb1")]
        for t in (2, 3):
            gather_a(0, ga1, t)
        nc.scalar.copy(b[SCALAR_B][:, 0:HJ], acc_for_scalar[:, 0:HJ])
        for t in range(PACK):
            gather_b(0, gb[t // 2], t)
        quantise_half(0, ga1, gb, "hid")

        ga1 = pair_tile("ga1_1", "ga1")
        gb = [pair_tile("gb0_1", "gb0"), pair_tile("gb1_1", "hid")]
        for t in (0, 1):
            gather_b(1, gb[0], t)
        for t in (2, 3):
            gather_a(1, ga1, t)
        for t in (2, 3):
            gather_b(1, gb[1], t)
        outcomes(0, 0, 1, nc.vector.tensor_copy)
        outcomes(0, 1, 4, nc.vector.tensor_copy)
        quantise_half(1, ga1, gb, "gb1")
        outcomes(1, 0, 4, nc.vector.tensor_copy)
        for k in range(4):
            scatter(k % 2, k // 2, 0)

        val = [tile(f"val{c}", [P, E], F32) for c in range(2)]
        gate = [tile(f"gate{c}", [P, E], F32) for c in range(2)]
        res = [tile(f"res{c}", [P, E], F32) for c in range(2)]

        def finish(c):
            nc.scalar.activation(val[c][:], page0[c][:].indirect(l6[:]), ACT.Copy, scale=se_t[:, c : c + 1])
            nc.scalar.activation(
                gate[c][:], page1[c][:].indirect(l7[:]), ACT.Sigmoid, bias=gf_t[:, c : c + 1], scale=sl_t[:, c : c + 1]
            )
            nc.vector.tensor_tensor(res[c][:], val[c][:], gate[c][:], ALU.mult)
            nc.sync.dma_start(out[P * c : P * (c + 1), :], res[c][:])

        for k in range(3):
            scatter(k % 2, k // 2, 1)
        finish(0)
        scatter(1, 1, 1)
        finish(1)
